import numpy as np, ml_dtypes
CORES = [16,18,20,22]
N = 4
BF = ml_dtypes.bfloat16
W, L, OR, ST, NEED = 4096, 256, 8, 3, 9
def forest(rng):
    o = np.argsort(rng.random((N, 8, 16, L, OR)), axis=2); k = np.arange(16).reshape(1, 1, 16, 1, 1)
    q = (rng.random(o.shape) * k).astype(np.int64); p = np.zeros_like(o)
    np.put_along_axis(p, o, np.take_along_axis(o, q, 2), 2)
    return np.where(rng.random(p.shape) < 0.1, k, p)
def limits(rng, lo, n):
    base = np.argsort(rng.random((N, 8, 1, L)), axis=-1) % n + lo
    return np.clip(base + rng.integers(-2, 3, (N, 8, 16, L)), 0, 15)
def parts(rng):
    x = rng.integers(0, 16, (N, 8, 16, W)); c = rng.integers(0, W, (N, 8, 16, L, OR)); p = forest(rng); a = limits(rng, 3, 8)
    v = rng.integers(0, 33, (N, 8, OR, L))
    o = np.arange(OR).reshape(1, 1, OR, 1); fav = rng.integers(0, OR, (1, 8, 1, L)); stick = rng.random((1, 8, 1, L)) < 0.5
    v = np.where(stick, np.where(o == fav, rng.integers(20, 33, v.shape), rng.integers(0, 7, v.shape)), v)
    return x, c, p, a, v
def bf(a): return np.ascontiguousarray(a).astype(np.float32).astype(BF)
def pack(x, c, p, a, v):
    return {"xt": bf(x.reshape(N, 128, W)), "pg": np.ascontiguousarray(c.reshape(N, 128, L * OR)).astype(np.int32), "pre": bf(p.reshape(N, 128, L * OR)),
            "lim": bf(a.reshape(N, 128, L)), "vv": np.ascontiguousarray(v.reshape(N, 8 * OR, L)).astype(np.int32)}
def setup_inputs(rng):
    return pack(*parts(rng))
def setup_inputs_ties(rng):
    x, c, p, a, v = parts(rng)
    dl = rng.integers(1, 8, (1, 8, 1, 1)); x = rng.integers(0, 9, (N, 8, 16, 1)) + dl * rng.integers(0, 2, x.shape)
    k = np.argsort(rng.random((N, 8, 1, L)), axis=-1) % 5; n = np.array([0, 2 * NEED - 16, 2 * NEED - 15, NEED - 1, 16])[k]
    a = np.where(np.argsort(rng.random(a.shape), axis=2) < n, dl, dl - 1)
    t = rng.choice(np.array([0, 1, 16, 31, 32]), (N, 8, 1, L))
    v = np.where(np.argsort(rng.random(v.shape), axis=2) < 2, t, np.minimum(rng.integers(0, 33, v.shape), t))
    return pack(x, c, p, a, v)
def setup_inputs_ends(rng):
    x, c, p, a, v = parts(rng)
    x = 15 * rng.integers(0, 2, x.shape); x[..., 0] = 0; x[..., W - 1] = 15
    e = rng.choice(np.array([0, 1, W // 2, W - 2, W - 1]), c.shape); c = np.where(rng.random((N, 8, 1, L, 1)) < 0.5, e, c)
    T = np.arange(16).reshape(1, 1, 16, 1, 1); k = rng.integers(0, 6, (N, 8, 1, L, 1))
    q = np.where(k == 0, T, np.where(k == 1, np.maximum(T - 1, 0), np.where(k == 2, 0, np.where(k == 3, 15, (T + 1) % 16))))
    p = np.where(k == 5, rng.integers(0, 16, p.shape), q)
    k = np.argsort(rng.random((N, 8, 1, L)), axis=-1) % 5; pos = np.argsort(rng.random(a.shape), axis=2)
    a = np.where(k == 0, 0, np.where(k == 1, 15, np.where(k == 2, 14, np.where(pos < np.where(k == 3, NEED, NEED - 1), 15, 0))))
    o = np.arange(OR).reshape(1, 1, OR, 1); k = rng.integers(0, 5, (N, 8, 1, L))
    v = np.where(k == 0, 0, np.where(k == 1, 32, np.where(k == 2, 32 * (o == 0), np.where(k == 3, 32 * (o == OR - 1), v))))
    z = int(rng.integers(0, 8)); w = np.argsort(rng.random(L)) % 4; x[:, z] = 15 * (np.arange(W) & 1)
    tt = T[0]; ring = (w == 0).reshape(1, 1, L, 1); climb = (w == 1).reshape(1, 1, L, 1)
    par = rng.integers(0, 2, (N, 1, L, OR)); even = c[:, z] - (c[:, z] & 1)
    c[:, z] = np.where(ring, even + ((par + tt) & 1), np.where(climb, even + ((par + (tt == 15)) & 1), c[:, z]))
    p[:, z] = np.where(ring, (tt + 1) % 16, np.where(climb, 0, p[:, z]))
    a = np.where(w == 1, 15, a); a[:, z] = np.where(w <= 1, 14 * rng.integers(0, 2, (N, 16, L)), a[:, z])
    v[:, z] = np.where(w == 1, 32 * (o[0] < 5) - 1 * (o[0] == 3), v[:, z])
    return pack(x, c, p, a, v)
def setup_inputs_alike(rng):
    x, c, p, a, v = parts(rng)
    x[:, ::2] = x[:, ::2][..., rng.integers(0, 8, W)]
    few = rng.integers(0, W, 5); few[0] = 0; few[1] = W - 1; c = few[rng.integers(0, 5, c.shape)]
    m = (rng.random((N, 8, 1, L, 1)) < 0.3) | (rng.random((N, 1, 1, L, 1)) < 0.3)
    c = np.where(m, c[:, :, :1], c); a[:, rng.integers(0, 8)] = 0
    return pack(x, c, p, a, v)
def setup_inputs_same(rng):
    x, c, p, a, v = parts(rng)
    o = np.arange(OR).reshape(1, 1, OR, 1); fav = rng.integers(0, OR, (1, 8, 1, L))
    v = np.where(o == fav, 32, rng.integers(0, 3, v.shape)); a = limits(rng, 5, 6)
    a[:, rng.integers(0, 8)] = rng.integers(0, 5, (N, 16, L))
    return pack(x, c, p, a, v)
def setup_inputs_spread(rng):
    x, c, p, a, v = parts(rng); E = np.array([0.25, 0.5, 1.0, 2.0, 4.0])
    def un(n, shape, by): return np.minimum((n * rng.random(shape) ** rng.choice(E, by)).astype(np.int64), n - 1)
    x = un(16, x.shape, (N, 8, 16, 1)); c = un(W, c.shape, (N, 8, 1, L, OR)); a = un(16, a.shape, (N, 8, 1, L)); v = un(33, v.shape, (N, 8, OR, 1))
    return pack(x, c, p, a, v)
def check_inputs(d):
    bad = []
    for k, hi in (("xt", 15), ("pg", W - 1), ("pre", 15), ("lim", 15), ("vv", 32)):
        b = np.asarray(d[k]).astype(np.float64)
        if not (np.min(b) >= 0 and np.max(b) <= hi and np.all(b == np.floor(b))): bad.append("range of " + k)
    return bad
def reference(xt, pg, pre, lim, vv):
    xs = np.ascontiguousarray(xt.astype(np.int32).reshape(N, 8, 16, W).transpose(0, 1, 3, 2))
    cur = np.ascontiguousarray(pg.astype(np.int64).reshape(N, 8, 16, L, OR).transpose(0, 1, 3, 4, 2))
    prd = np.ascontiguousarray(pre.astype(np.int64).reshape(N, 8, 16, L, OR).transpose(0, 1, 3, 4, 2))
    a = np.ascontiguousarray(lim.astype(np.int32).reshape(N, 8, 16, L).transpose(0, 1, 3, 2))
    v = np.ascontiguousarray(vv.astype(np.int64).reshape(N, 8, OR, L).transpose(0, 1, 3, 2))
    m = np.zeros((N, 8, L), np.int64)
    g0 = np.arange(8).reshape(1, 8, 1); l0 = np.arange(L).reshape(1, 1, L)
    for s in range(N):
        h = ((np.arange(N) + s) % N).reshape(N, 1, 1)
        o = np.argmax(v, axis=3)
        c = cur[h, g0, l0, o]; p = prd[h, g0, l0, o]
        got = np.zeros((N, 8, L), np.int64)
        for t in range(ST):
            F = xs[h[..., None], g0[..., None], c]
            G = np.take_along_axis(F, p[..., None], 3)
            D = np.abs(F - G)
            ok = np.add.reduce((D <= a[:, :, :, None, :]).astype(np.int64), axis=4) >= NEED
            full = np.all(ok, axis=3)
            got = got + full
            c = np.where(full[..., None], (5 * c + 1) & (W - 1), np.where(ok, c, (5 * c + np.add.reduce(D, axis=4) + 1) & (W - 1)))
        cur[h, g0, l0, o] = c
        m = m + got
        odd = np.add.reduce(got, axis=1, keepdims=True) & 1
        v = v + 1 + odd[..., None]
        np.put_along_axis(v, o[..., None], np.add.reduce(ok.astype(np.int64), axis=3)[..., None], 3)
    return {"yg": np.ascontiguousarray(cur.transpose(0, 1, 4, 2, 3)).reshape(N, 128, L * OR).astype(np.float32),
            "yv": np.ascontiguousarray(v.transpose(0, 1, 3, 2)).reshape(N, 8 * OR, L).astype(np.float32), "ym": m.astype(np.float32)}

from concourse.mybir import AluOpType, ActivationFunctionType

ACT = ActivationFunctionType
NS, ST = 4, 3
H, J = 2, 2
LH, LB = 128, 64
NK = LH // 16
KW = 8 * NK
KG = KW + NK
FW = ST * NK
BIG = 65536
OFF = 491520

SCRATCH = {
    "X": ("sbuf", [128, 4096], "bfloat16"),
    "vvi": ("sbuf", [64, 256], "int32"), "vvb": ("sbuf", [64, 256], "bfloat16"), "R": ("sbuf", [64, 2048], "bfloat16"),
    "limb": ("sbuf", [128, 256], "bfloat16"),
    "ones": ("sbuf", [128, 2048], "bfloat16"), "E": ("sbuf", [128, 2048], "bfloat16"),
    "gA": ("sbuf", [128, 128], "bfloat16"), "gm": ("sbuf", [128, 128], "bfloat16"), "okw": ("sbuf", [128, 128], "bfloat16"),
    "g8A": ("sbuf", [64, 128], "bfloat16"), "g8m": ("sbuf", [64, 128], "bfloat16"), "g8s": ("sbuf", [64, 128], "bfloat16"),
    "vsel": ("sbuf", [64, 2048], "bfloat16"),
    "identb": ("sbuf", [128, 128], "bfloat16"), "negi": ("sbuf", [128, 128], "bfloat16"), "identf": ("sbuf", [128, 128], "float32"),
    "fsel1": ("sbuf", [128, 128], "bfloat16"), "fsel": ("sbuf", [128, 128], "bfloat16"),
    "sel1": ("sbuf", [128, 2048], "bfloat16"), "sel2": ("sbuf", [128, 2048], "bfloat16"),
    "pm": ("sbuf", [128, 128], "int32"), "pm2": ("sbuf", [128, 128], "int32"), "sameb": ("sbuf", [128, 128], "bfloat16"),
    "om": ("sbuf", [64, 8], "int32"), "om2": ("sbuf", [64, 8], "int32"), "omask": ("sbuf", [64, 8], "float32"),
    "pc4": ("sbuf", [128, 4], "int32"), "pc15": ("sbuf", [128, 4], "int32"), "pc8": ("sbuf", [128, 4], "float32"),
    "pc7": ("sbuf", [128, 4], "int32"), "rep": ("sbuf", [128, 4], "uint16"),
    "kc": ("sbuf", [128, KW], "int32"), "keyc": ("sbuf", [128, KW], "int32"),
    "limT": ("sbuf", [128, NS * 256], "bfloat16"),
    "keys": ("sbuf", [128, (NS + 1) * H * KG], "int32"),
    "pay": ("sbuf", [128, NS * H * KG], "int32"),
    "fx": ("sbuf", [128, NS * H * FW], "bfloat16"),
    "fl": ("sbuf", [128, NS * H * FW], "bfloat16"),
    "PA0": ("psum", [128, 1024], "float32"), "PA1": ("psum", [128, 1024], "float32"),
    "PP0": ("psum", [128, 512], "float32"), "PP1": ("psum", [128, 512], "float32"),
    "PN0": ("psum", [128, 512], "float32"), "PN1": ("psum", [128, 512], "float32"),
}
for _h in range(H):
    for _n, _w, _d in (("pgi", 1024, "int32"), ("pgw", 1024, "float32"), ("prew", 1024, "float32"), ("mA", KW // 2, "int32"), ("mB", KW // 4, "int32"),
                       ("km", NK, "int32"), ("li", NK, "int32"), ("lst", NK, "uint16"), ("ea", NK, "int32"), ("eb", NK, "int32"),
                       ("eq", KW, "float32"), ("cfl", LH, "float32"), ("c16", LH, "uint16"), ("p16", LH, "uint16"), ("u5", LH, "float32"),
                       ("ci", LH, "int32"), ("cpp", LH, "int32"), ("qq", LH, "float32"), ("sg", ST * LH, "bfloat16"), ("nk1", NK, "float32"),
                       ("mi", NK, "int32"), ("od", NK, "int32"), ("xx", NK, "float32"), ("dl", NK, "float32"), ("em", KW, "float32"),
                       ("hi", KW, "int32"), ("fv", KW, "bfloat16"), ("yb", NK, "bfloat16")):
        SCRATCH["%s%d" % (_n, _h)] = ("sbuf", [128, _w], _d)
    SCRATCH["yvs%d" % _h] = ("sbuf", [8, 1024], "float32")
    SCRATCH["yms%d" % _h] = ("sbuf", [8, LH], "float32")
    for _j in range(J):
        for _n in ("F", "F2", "D", "AD", "ni"):
            SCRATCH["%s%d%d" % (_n, _h, _j)] = ("sbuf", [128, 16 * LB], "bfloat16")

SEMAPHORES = ["cV", "cS", "cP", "cG", "lvv", "llim", "lxt", "lpg0", "lpg1", "lpre0", "lpre1", "outs", "sent"]
SEMAPHORES += ["alim%d" % s for s in range(1, NS)] + ["akey%d%d" % (s, h) for s in range(1, NS + 1) for h in range(H)]
SEMAPHORES += ["afl%d" % x for x in range(H, H * NS)]

CYC, PEC = 0.83, 0.42
GAT = 1.5
VFIX, SFIX, PFIX = 60, 80, 0


def WAY(s, st, h, j):
    return "PS"[j]


def graph(ctx):
    T, A = ctx["T"], AluOpType
    NE = ctx["X"]
    ops = []

    def add(eng, cost, rd, wr, fn, pr=0.0, pool=None, free=None, sem=None, inc=None, lat=0.0, bk=(0,)):
        ops.append(dict(eng=eng, cost=cost, rd=rd, wr=wr, fn=fn, pr=pr, pool=pool, free=free, sem=sem, inc=inc, lat=lat, bk=bk))

    def V(n, cyc, rd, wr, fn, **k):
        add("V", VFIX + max(64, n * cyc) * CYC, rd, wr, fn, **k)

    def S(n, cyc, rd, wr, fn, **k):
        add("S", SFIX + max(64, n * cyc) * CYC, rd, wr, fn, **k)

    def P(k, n, rd, wr, fn, **kw):
        add("P", k * (PFIX + max(64, n) * PEC), rd, wr, fn, **kw)

    def G(n, rd, wr, fn, **k):
        add("G", 150 + 2 * n * CYC, rd, wr, fn, **k)

    def load(eng, out, inp, tile, sem, lat, pr):
        add(eng, 80, [], [tile], lambda e, p: e.dma_start(out, inp), pr=pr, sem=sem, inc=16, lat=lat)

    def kv(s, h, a, b):
        return T.keys[:, (H * s + h) * KG + a:(H * s + h) * KG + b]

    load("Q", T.vvi[:], T.vv[:], "vvi", "lvv", 2200, -9.0)
    load("Q", T.pgi0[:], T.pg[:, 0:1024], "pgi0", "lpg0", 4000, -8.9)
    load("S", T.X[:], T.xt[:], "X", "lxt", 7500, -9.0)
    load("Q", T.limb[:], T.lim[:], "limb", "llim", 3000, -8.8)
    load("Q", T.pgi1[:], T.pg[:, 1024:2048], "pgi1", "lpg1", 9500, -8.7)

    def pre_fill(h):
        G(1024, [], ["prew%d" % h], lambda e, p: e.iota(T["prew%d" % h][:], [[0, 2], [16, 64], [0, 8]], 0, 0, allow_small_or_imprecise_dtypes=True), pr=-9.0 + 3 * h)
        add("G", 1100, ["prew%d" % h], ["prew%d" % h], lambda e, p: e.dma_start(T["prew%d" % h][:], T.pre[:, 1024 * h:1024 * h + 1024], accum_op=A.add),
            pr=-8.9 + 3 * h, sem="lpre%d" % h, inc=16, lat=4000)

    V(128, 0.5, [], ["ones"], lambda e, p: e.memset(T.ones[:, 0:128], 1.0), pr=-9.5)
    V(1920, 0.5, [], ["onesE"], lambda e, p: e.memset(T.ones[:, 128:2048], 1.0), pr=-8.0)
    G(8, [], ["om"], lambda e, p: e.iota(T.om[:], [[-1, 8]], 8, 1), pr=-9.9)
    G(4, [], ["pc4"], lambda e, p: e.iota(T.pc4[:], [[0, 4]], 0, 1), pr=-9.8)
    G(KW, [], ["kc"], lambda e, p: e.iota(T.kc[:], [[1, 8], [128, NK]], 0, 0), pr=-9.7)
    V(8, 1, ["om"], ["om2"], lambda e, p: e.tensor_scalar(T.om2[:], T.om[:], 7, None, A.bitwise_and), pr=-9.0)
    V(8, 1, ["om2"], ["omask"], lambda e, p: e.tensor_scalar(T.omask[:], T.om2[:], 0.0, None, A.is_equal), pr=-9.0)
    V(4, 1, ["pc4"], ["pc15"], lambda e, p: e.tensor_scalar(T.pc15[:], T.pc4[:], 15, None, A.bitwise_and), pr=-9.0)
    V(4, 1, ["pc15"], ["pc8"], lambda e, p: e.tensor_scalar(T.pc8[:], T.pc15[:], 8.0, None, A.mult), pr=-9.0)
    V(4, 1, ["pc4"], ["pc7"], lambda e, p: e.tensor_scalar(T.pc7[:], T.pc4[:], 7, None, A.bitwise_and), pr=-7.0)
    V(4, 1, ["pc7"], ["rep"], lambda e, p: e.tensor_copy(T.rep[:], T.pc7[:]), pr=-7.0)
    V(KW, 1, ["kc", "pc8"], ["keyc"], lambda e, p: e.tensor_scalar(T.keyc[:], T.kc[:], T.pc8[:, 0:1], None, A.add), pr=-9.0)
    G(128, ["ones"], ["g8A"], lambda e, p: e.affine_select(T.g8A[:], T.ones[0:64, 0:128], [[-8, 8], [0, 16]], A.is_ge, 0.0, 0, 1), pr=-9.6)
    G(128, ["g8A"], ["g8m"], lambda e, p: e.affine_select(T.g8m[:], T.g8A[:], [[8, 8], [0, 16]], A.is_ge, 0.0, 7, -1), pr=-9.5)
    S(128, 1, ["g8m"], ["g8s"], lambda e, p: e.activation(T.g8s[:], T.g8m[:], ACT.Copy, scale=-1024.0), pr=-9.0)
    V(2048, 0.5, [], ["vsel"], lambda e, p: e.memset(T.vsel[:], 0.0), pr=-9.2)
    for k in range(8):
        V(16, 1, ["g8s"], ["vsel"], lambda e, p, k=k: e.tensor_copy(T.vsel[:, 16 * k:2048:129], T.g8s[:, 16 * k:16 * k + 16]), pr=-9.0)
    pre_fill(0)
    V(256, 1, ["vvi"], ["vvb"], lambda e, p: e.tensor_copy(T.vvb[:], T.vvi[:]), pr=-9.0)
    for h in range(H):
        for o in range(8):
            V(128, 0.5, ["vvb", "omask"], ["R%d" % h],
              lambda e, p, h=h, o=o: e.tensor_scalar(T.R[:, 1024 * h + 128 * o:1024 * h + 128 * o + 128], T.vvb[:, 128 * h:128 * h + 128], T.omask[:, o:o + 1], None, A.mult),
              pr=-9.0 + 2 * h)

        def vmm(e, p, h=h):
            for b in range(16):
                i = e.matmul(p[:, 0:KW], T.vsel[:, 128 * b:128 * b + 128], T.R[:, 1024 * h + b:1024 * h + 1024:16], b == 0, b == 15)
            return i
        P(16, KW, ["vsel", "R%d" % h], ["vP%d" % h], vmm, pr=-9.0 + 2 * h, pool=("N", "vP%d" % h))
        V(KW, 1, ["vP%d" % h, "keyc"], ["key0%d" % h], lambda e, p, h=h: e.tensor_tensor(kv(0, h, 0, KW), p[:, 0:KW], T.keyc[:], A.add),
          pr=-9.0 + 2 * h, pool=("N", "vP%d" % h), free=1)
        V(NK, 1, [], ["gro0%d" % h], lambda e, p, h=h: e.memset(kv(0, h, KW, KG), 0), pr=-8.0 + 2 * h)
        V(1024, 1, ["pgi%d" % h], ["pgw%d" % h], lambda e, p, h=h: e.tensor_copy(T["pgw%d" % h][:], T["pgi%d" % h][:]), pr=-8.0 + 3 * h)
    G(128, ["ones"], ["identb"], lambda e, p: e.affine_select(T.identb[:], T.ones[:, 0:128], [[-1, 128]], A.is_equal, 0.0, 0, 1), pr=-8.5)
    S(128, 1, ["identb"], ["negi"], lambda e, p: e.activation(T.negi[:], T.identb[:], ACT.Copy, scale=-1.0), pr=-7.0)
    S(128, 1, ["identb"], ["identf"], lambda e, p: e.activation(T.identf[:], T.identb[:], ACT.Copy), pr=-7.0)
    G(128, ["ones"], ["gA"], lambda e, p: e.affine_select(T.gA[:], T.ones[:, 0:128], [[-16, 8], [0, 16]], A.is_ge, 0.0, 0, 1), pr=-8.4)
    G(128, ["gA"], ["gm"], lambda e, p: e.affine_select(T.gm[:], T.gA[:], [[16, 8], [0, 16]], A.is_ge, 0.0, 15, -1), pr=-8.3)
    S(128, 1, ["gm"], ["okw"], lambda e, p: e.activation(T.okw[:], T.gm[:], ACT.Copy, scale=float(OFF // 16)), pr=-7.0)
    V(2048, 0.5, [], ["sel1"], lambda e, p: e.memset(T.sel1[:], 0.0), pr=-8.0)
    for k in range(8):
        V(16, 1, ["gm"], ["sel1"], lambda e, p, k=k: e.tensor_copy(T.sel1[:, 16 * k:2048:129], T.gm[:, 16 * k:16 * k + 16]), pr=-7.5)
    S(2048, 1, ["sel1"], ["sel2"], lambda e, p: e.activation(T.sel2[:], T.sel1[:], ACT.Copy, scale=float(BIG)), pr=-7.5)

    def lmm(e, p):
        e.matmul(p[:, 0:128], T.limb[:, 0:128], T.identb[:], True, True)
        return e.matmul(p[:, 128:256], T.limb[:, 128:256], T.identb[:], True, True)
    P(2, 128, ["limb", "identb"], ["lP"], lmm, pr=-7.5, pool=("N", "lP"))
    S(256, 1, ["lP"], ["limT0"], lambda e, p: e.activation(T.limT[:, 0:256], p[:, 0:256], ACT.Copy), pr=-7.4, pool=("N", "lP"), free=1)
    G(2048, ["ones", "onesE"], ["E"], lambda e, p: e.affine_select(T.E[:], T.ones[:], [[-1, 128], [0, 16]], A.is_equal, 0.0, 0, 1), pr=-7.5)
    pre_fill(1)
    G(128, [], ["pm"], lambda e, p: e.iota(T.pm[:], [[-1, 128]], 2048, 1), pr=-5.5)
    V(128, 1, ["pm"], ["pm2"], lambda e, p: e.tensor_scalar(T.pm2[:], T.pm[:], 15, None, A.bitwise_and), pr=0.5)
    V(128, 1, ["pm2"], ["sameb"], lambda e, p: e.tensor_scalar(T.sameb[:], T.pm2[:], 0.0, 1024.0, A.is_equal, A.mult), pr=0.5)
    for s in range(1, NS):
        add("G", 500, ["limT0"], [], lambda e, p, s=s: ctx["send"](s, T.limT[:, 256 * s:256 * s + 256], T.limT[:, 0:256], "alim%d" % s), pr=-5.0, sem="sent", inc=NE, lat=2500)
        add("W", 0, [], ["limT%d" % s], None, sem="alim%d" % s, inc=NE, lat=15000)
    G(128, ["ones"], ["fsel1"], lambda e, p: e.affine_select(T.fsel1[:], T.ones[:, 0:128], [[-1, 16], [-16, 8]], A.is_equal, 0.0, 0, 1), pr=-4.0)
    S(128, 1, ["fsel1"], ["fsel"], lambda e, p: e.activation(T.fsel[:], T.fsel1[:], ACT.Copy, scale=1.0 / 1024.0), pr=1.5)

    def begin(s, h):
        pr = ST * s - 0.6 + 0.5 * h
        kt, gt = "key%d%d" % (s, h), ("gro0%d" % h if s == 0 else "key%d%d" % (s, h))
        n = lambda x: "%s%d" % (x, h)
        t = lambda x: T["%s%d" % (x, h)]
        V(KW // 2, 2, [kt], [n("mA")], lambda e, p: e.tensor_tensor(t("mA")[:], kv(s, h, 0, KW // 2), kv(s, h, KW // 2, KW), A.min), pr=pr)
        V(KW // 4, 2, [n("mA")], [n("mB")], lambda e, p: e.tensor_tensor(t("mB")[:], t("mA")[:, 0:KW // 4], t("mA")[:, KW // 4:KW // 2], A.min), pr=pr)
        V(NK, 2, [n("mB")], [n("km")], lambda e, p: e.tensor_tensor(t("km")[:], t("mB")[:, 0:NK], t("mB")[:, NK:2 * NK], A.min), pr=pr)
        V(NK, 1, [n("km")], [n("li")], lambda e, p: e.tensor_scalar(t("li")[:], t("km")[:], 1023, None, A.bitwise_and), pr=pr)
        V(NK, 1, [n("li")], [n("lst")], lambda e, p: e.tensor_copy(t("lst")[:], t("li")[:]), pr=pr)
        V(LH, GAT, [n("pgw"), n("lst")], ["c16%d%d" % (h, j) for j in range(J)], lambda e, p: e.tensor_copy(t("c16")[:], t("pgw")[:].indirect(t("lst")[:])), pr=pr)
        S(LH, GAT, [n("pgw"), n("lst")], [n("cfl")], lambda e, p: e.activation(t("cfl")[:], t("pgw")[:].indirect(t("lst")[:]), ACT.Copy), pr=pr + .02)
        V(LH, GAT, [n("prew"), n("lst")], [n("p16")], lambda e, p: e.tensor_copy(t("p16")[:], t("prew")[:].indirect(t("lst")[:])), pr=pr + .01)
        S(LH, 1, [n("cfl")], ["u5%d%d" % (h, j) for j in range(J)], lambda e, p: e.activation(t("u5")[:], t("cfl")[:], ACT.Identity, scale=5.0, bias=float(1 - OFF)), pr=pr + .3)
        V(NK, 2, [gt, n("km")], [n("ea")], lambda e, p: e.tensor_tensor(t("ea")[:], kv(s, h, KW, KG), t("km")[:], A.subtract), pr=pr + .9)
        V(NK, 2, [n("ea"), n("li")], [n("eb")], lambda e, p: e.tensor_tensor(t("eb")[:], t("ea")[:], t("li")[:], A.add), pr=pr + .9)
        V(KW, GAT, [n("km"), kt, "rep"], [n("eq")], lambda e, p: e.tensor_tensor(t("eq")[:], t("km")[:].indirect(T.rep[:]), kv(s, h, 0, KW), A.is_equal), pr=pr + .9)

    def step(s, st, h, j):
        pr = ST * s + st + 0.5 * h + 0.25 * j
        x = "%d%d" % (h, j)
        a, b = LB * j, LB * j + LB
        F, F2, D, AD, ni = T["F" + x], T["F2" + x], T["D" + x], T["AD" + x], T["ni" + x]
        t = lambda n: T["%s%d" % (n, h)][:, a:b]
        sg = T["sg%d" % h][:, LH * st + a:LH * st + b]
        sgt = "sg%s%d" % (x, st)
        kA, kD, kP, kN = "A%s" % x, "D%s" % x, "P%s" % x, "N%s" % x
        cin, cint = (t("cfl"), "cfl%d" % h) if st == 0 else (t("ci"), "ci" + x)
        last = st == ST - 1
        n16 = 16 * LB
        S(n16, GAT, ["X", "c16" + x], ["F" + x], lambda e, p: e.activation(F[:], T.X[:].indirect(t("c16")), ACT.Copy), pr=pr)

        def dfm(e, p, c):
            e.matmul(p[:, 512 * c:512 * c + 512], T.identb[:], F[:, 512 * c:512 * c + 512], True, False)
            return e.matmul(p[:, 512 * c:512 * c + 512], T.negi[:], D[:, 512 * c:512 * c + 512], False, True)
        if WAY(s, st, h, j) == "P":
            V(n16, GAT, ["F" + x, "p16%d" % h], ["D" + x], lambda e, p: e.tensor_copy(D[:], F[:].indirect(t("p16"))), pr=pr)
            for c in range(2):
                P(2, 512, ["F" + x, "D" + x, "identb", "negi"], ["%s_%d" % (kD, c)], lambda e, p, c=c: dfm(e, p, c), pr=pr - .2, pool=("A", kD), bk=(c,))
            S(n16, 1, ["%s_0" % kD, "%s_1" % kD], ["AD" + x], lambda e, p: e.activation(AD[:], p[:], ACT.Abs), pr=pr, pool=("A", kD), free=1, bk=(0, 1))
        else:
            S(n16, 1, ["F" + x], ["F2" + x], lambda e, p: e.activation(F2[:], F[:], ACT.Copy), pr=pr)
            V(n16, GAT, ["F" + x, "F2" + x, "p16%d" % h], ["D" + x], lambda e, p: e.tensor_tensor(D[:], F2[:].indirect(t("p16")), F[:], A.subtract), pr=pr)
            S(n16, 1, ["D" + x], ["AD" + x], lambda e, p: e.activation(AD[:], D[:], ACT.Abs), pr=pr)
        for c in range(2):
            P(1, 512, ["limT%d" % s, "E", "D" + x], ["%s_%d" % (kA, c)],
              lambda e, p, c=c: e.matmul(p[:, 512 * c:512 * c + 512], T.limT[:, 256 * s + LH * h:256 * s + LH * h + LH],
                                         T.E[:, n16 * j + 512 * c:n16 * j + 512 * c + 512], True, True),
              pr=pr + 0.3, pool=("A", kA), bk=(c,))
        V(n16, 1, ["AD" + x, kA + "_0", kA + "_1"], ["ni" + x], lambda e, p: e.tensor_tensor(ni[:], AD[:], p[:], A.is_gt), pr=pr, pool=("A", kA), free=1, bk=(0, 1))

        def adm(e, p):
            e.matmul(p[:, 0:LB], T.identf[:], t("u5"), True, False)
            for k in range(16):
                i = e.matmul(p[:, 0:LB], T.sel1[:, 128 * k:128 * k + 128], AD[:, k:n16:16], False, False)
            return i

        def nim(e, p):
            for k in range(16):
                i = e.matmul(p[:, 0:LB], T.sel2[:, 128 * k:128 * k + 128], ni[:, k:n16:16], False, k == 15)
            return i
        P(20, LB, ["AD" + x, "u5" + x, "identf", "sel1"], [kP], adm, pr=pr + 0.2, pool=("P", kP))
        P(16, LB, ["ni" + x, "sel2"], [kP], nim, pr=pr, pool=("P", kP))
        S(LB, 1, [kP], [sgt], lambda e, p: e.activation(sg, p[:, 0:LB], ACT.Sign, scale=-1.0), pr=pr - .5, pool=("P", kP), free=2)
        V(LB, 1, [kP, cint], ["qq" + x], lambda e, p: e.tensor_tensor(t("qq"), p[:, 0:LB], cin, A.max), pr=pr - .5, pool=("P", kP), free=2)

        def okm(e, p):
            e.matmul(p[:, 0:LB], T.identf[:], t("u5"), True, False)
            return e.matmul(p[:, 0:LB], T.okw[:], sg, False, True)
        P(5, LB, [sgt, "u5" + x, "okw", "identf"], [kN], okm, pr=pr - .5, pool=("N", kN))
        V(LB, 1, [kN, "qq" + x], ["cpp" + x], lambda e, p: e.tensor_tensor(t("cpp"), p[:, 0:LB], t("qq"), A.max), pr=pr - .5, pool=("N", kN), free=1)
        V(LB, 1, ["cpp" + x], ["ci" + x], lambda e, p: e.tensor_scalar(t("ci"), t("cpp"), 4095, None, A.bitwise_and), pr=pr - .5)
        if not last:
            V(LB, 1, ["ci" + x], ["c16" + x], lambda e, p: e.tensor_copy(t("c16"), t("ci")), pr=pr - .5)
            V(LB, 1, ["ci" + x], ["u5" + x], lambda e, p: e.tensor_scalar(t("u5"), t("ci"), 5.0, float(1 - OFF), A.mult, A.add), pr=pr - .4)

    def end(s, h):
        pr = ST * (s + 1) - 1.0 + 0.5 * h
        q = H * s + h
        n = lambda x: "%s%d" % (x, h)
        t = lambda x: T["%s%d" % (x, h)]
        kt, gt = "key%d%d" % (s, h), ("gro0%d" % h if s == 0 else "key%d%d" % (s, h))
        pay = lambda a, b: T.pay[:, KG * q + a:KG * q + b]
        fx = lambda a, b: T.fx[:, FW * q + a:FW * q + b]
        kL = "L%d" % h

        def lpm(e, p):
            for b in range(16):
                i = e.matmul(p[:, 0:FW], T.sel1[:, 128 * b:128 * b + 128], t("sg")[:, b:ST * LH:16], b == 0, b == 15)
            return i

        def mpm(e, p):
            for k in range(ST):
                i = e.matmul(p[:, 64:64 + NK], T.sameb[:], fx(NK * k, NK * k + NK), k == 0, k == ST - 1)
            return i
        P(16, FW, ["sg%d%d%d" % (h, j, k) for j in range(J) for k in range(ST)] + ["sel1"], [kL], lpm, pr=pr, pool=("N", kL))
        S(FW, 1, [kL], ["fx%d" % q], lambda e, p: e.activation(fx(0, FW), p[:, 0:FW], ACT.Relu, bias=-15.0), pr=pr, pool=("N", kL))
        S(NK, 1, [kL], [n("nk1")], lambda e, p: e.activation(t("nk1")[:], p[:, FW - NK:FW], ACT.Identity, scale=-512.0, bias=float(1024 * (s + 1) - 8192)), pr=pr, pool=("N", kL))
        P(3, NK, ["fx%d" % q, "sameb"], [kL], mpm, pr=pr, pool=("N", kL))
        V(NK, 1, [kL], [n("mi")], lambda e, p: e.tensor_copy(t("mi")[:], p[:, 64:64 + NK]), pr=pr, pool=("N", kL), free=1)
        V(NK, 1, [n("mi")], [n("od")], lambda e, p: e.tensor_scalar(t("od")[:], t("mi")[:], 1024, None, A.bitwise_and), pr=pr)
        V(NK, 2, [n("nk1"), n("od")], [n("xx")], lambda e, p: e.tensor_tensor(t("xx")[:], t("nk1")[:], t("od")[:], A.add), pr=pr)
        V(NK, 2, [n("xx"), n("eb")], [n("dl")], lambda e, p: e.tensor_tensor(t("dl")[:], t("xx")[:], t("eb")[:], A.add), pr=pr)
        V(NK, 2, [gt, n("od")], ["payg%d" % q], lambda e, p: e.tensor_tensor(pay(KW, KG), kv(s, h, KW, KG), t("od")[:], A.add), pr=pr)
        V(KW, GAT, [n("dl"), n("eq"), "rep"], [n("em")], lambda e, p: e.tensor_tensor(t("em")[:], t("dl")[:].indirect(T.rep[:]), t("eq")[:], A.mult), pr=pr)
        V(KW, 2, [kt, n("em")], ["pay%d" % q], lambda e, p: e.tensor_tensor(pay(0, KW), kv(s, h, 0, KW), t("em")[:], A.add), pr=pr)
        add("G", 500, ["pay%d" % q, "payg%d" % q], ["snd%d" % q], lambda e, p: ctx["send"](1, kv(s + 1, h, 0, KG), pay(0, KG), "akey%d%d" % (s + 1, h)), pr=pr - 2, sem="sent", inc=NE, lat=2000)
        add("W", 0, ["snd%d" % q], ["key%d%d" % (s + 1, h)], None, sem="akey%d%d" % (s + 1, h), inc=NE, lat=600)
        if s:
            add("G", 500, ["fx%d" % q], ["sndf%d" % q], lambda e, p: ctx["send"](-s, T.fl[:, FW * q:FW * q + FW], fx(0, FW), "afl%d" % q), pr=pr, sem="sent", inc=NE, lat=2000)
            add("W", 0, ["sndf%d" % q], ["fl%d" % q], None, sem="afl%d" % q, inc=NE, lat=600)
        V(LH, 3.5, [n("lst")] + ["ci%d%d" % (h, j) for j in range(J)], [n("pgw")], lambda e, p: e.tensor_copy(t("pgw")[:].indirect(t("lst")[:]), t("ci")[:]), pr=pr + .05)

    def final(h):
        pr = ST * NS + 0.5 * h
        n = lambda x: "%s%d" % (x, h)
        t = lambda x: T["%s%d" % (x, h)]
        kt = "key%d%d" % (NS, h)
        add("Q", 80, [n("pgw")], [], lambda e, p: e.dma_start(T.yg[:, 1024 * h:1024 * h + 1024], t("pgw")[:]), pr=pr, sem="outs", inc=16, lat=4000)
        V(KW, 2, [kt, "keyc"], [n("hi")], lambda e, p: e.tensor_tensor(t("hi")[:], kv(NS, h, 0, KW), T.keyc[:], A.subtract), pr=pr - 3)
        V(KW, GAT, [kt, n("hi"), "rep"], [n("fv")], lambda e, p: e.tensor_tensor(t("fv")[:], kv(NS, h, KW, KG).indirect(T.rep[:]), t("hi")[:], A.subtract), pr=pr - 3)
        for c in range(2):
            def fvm(e, p, c=c):
                for b in range(16):
                    i = e.matmul(p[0:8, 512 * c + b:512 * c + 512:16], T.fsel[:, 8 * b:8 * b + 8], t("fv")[:, 32 * c:32 * c + 32], True, True)
                return i
            P(16, 32, [n("fv"), "fsel"], ["Y%d_%d" % (h, c)], fvm, pr=pr - 3, pool=("A", "Y%d" % h), bk=(c,))
        V(512, 1, ["Y%d_0" % h], ["yvsA%d" % h], lambda e, p: e.tensor_scalar(t("yvs")[:, 0:512], p[0:8, 0:512], float(NS), None, A.add), pr=pr - 3, pool=("A", "Y%d" % h), free=2)
        S(512, 1, ["Y%d_1" % h], ["yvsB%d" % h], lambda e, p: e.activation(t("yvs")[:, 512:1024], p[0:8, 512:1024], ACT.Identity, bias=float(NS)), pr=pr - 3, pool=("A", "Y%d" % h), free=2, bk=(1,))
        add("Q", 80, ["yvsA%d" % h, "yvsB%d" % h], [], lambda e, p: e.dma_start(T.yv[:, LH * h:LH * h + LH], t("yvs")[:]), pr=pr - 3, sem="outs", inc=16, lat=2200)
        kM = "M%d" % h

        def ysum(e, p):
            for i in range(NS):
                for k in range(ST):
                    c = FW * (H * i + h) + NK * k
                    r = e.matmul(p[:, 0:NK], T.identb[:], (T.fl if i else T.fx)[:, c:c + NK], i + k == 0, i == NS - 1 and k == ST - 1)
            return r

        def ymm(e, p):
            for b in range(16):
                r = e.matmul(p[0:8, 128 + b:256:16], T.fsel1[:, 8 * b:8 * b + 8], t("yb")[:], True, True)
            return r
        P(12, NK, ["fx%d" % h, "identb"] + ["fl%d" % (H * s + h) for s in range(1, NS)], [kM], ysum, pr=pr - 2, pool=("N", kM))
        S(NK, 1, [kM], [n("yb")], lambda e, p: e.activation(t("yb")[:], p[:, 0:NK], ACT.Copy), pr=pr - 2, pool=("N", kM))
        P(16, NK, [n("yb"), "fsel1"], [kM], ymm, pr=pr - 2, pool=("N", kM))
        S(LH, 1, [kM], [n("yms")], lambda e, p: e.activation(t("yms")[:], p[0:8, 128:256], ACT.Copy), pr=pr - 2, pool=("N", kM), free=1)
        add("Q", 80, [n("yms")], [], lambda e, p: e.dma_start(T.ym[:, LH * h:LH * h + LH], t("yms")[:]), pr=pr - 2, sem="outs", inc=16, lat=2200)

    for s in range(NS):
        for h in range(H):
            begin(s, h)
            for st in range(ST):
                for j in range(J):
                    step(s, st, h, j)
            end(s, h)
    for h in range(H):
        final(h)
    return ops


POOLS = {"A": ("PA0", "PA1"), "P": ("PP0", "PP1"), "N": ("PN0", "PN1")}
WAKE = 100.0
LS, LB0 = 0.0, 0.0


def deps_of(ops, order):
    last, readers, out = {}, {}, {}
    for i in order:
        o, d = ops[i], set()
        for r in o["rd"]:
            if r in last:
                d.add(last[r])
        for w in o["wr"]:
            if w in last:
                d.add(last[w])
            d.update(readers.get(w, ()))
        d.discard(i)
        out[i] = d
        for r in o["rd"]:
            readers.setdefault(r, []).append(i)
        for w in o["wr"]:
            last[w] = i
            readers[w] = []
    return out


def plan(ops):
    n = len(ops)
    dep = deps_of(ops, range(n))
    succ = [[] for _ in range(n)]
    need = [len(dep[i]) for i in range(n)]
    for i in range(n):
        for d in dep[i]:
            succ[d].append(i)
    done, start, buf = [0.0] * n, [0.0] * n, {}
    free = {e: 0.0 for e in "VSPGQW"}
    slot = {k: [0.0] * len(v) for k, v in POOLS.items()}
    held, fin = {}, {}
    ready = [i for i in range(n) if not need[i]]
    order = []
    while ready:
        best = {}
        for i in ready:
            o = ops[i]
            t = free[o["eng"]] if o["eng"] != "W" else 0.0
            for d in dep[i]:
                t = max(t, done[d] + (0.0 if o["eng"] == "W" or ops[d]["eng"] == "P" and o["eng"] == "P" else WAKE))
            if o["pool"] and o["pool"] not in held:
                fr = [x for x in slot[o["pool"][0]] if x is not None]
                if not fr:
                    continue
                t = max(t, min(fr))
            best.setdefault(o["eng"], []).append((t, i))
        cand = None
        for e, lst in best.items():
            t0 = min(lst)[0] + LB0
            pick = min((ops[i]["pr"], t, i) for t, i in lst if t <= t0 + (LS if ops[i]["cost"] < 260 else 0))
            if cand is None or pick[1] < cand[0]:
                cand = (pick[1], pick[2])
        t, i = cand
        o = ops[i]
        ready.remove(i)
        if o["pool"]:
            k = o["pool"]
            if k not in held:
                fr = [(x, y) for y, x in enumerate(slot[k[0]]) if x is not None]
                held[k] = min(fr)[1]
                slot[k[0]][held[k]] = None
            buf[i] = POOLS[k[0]][held[k]]
        start[i] = t
        done[i] = t + o["cost"] + o["lat"]
        free[o["eng"]] = t + o["cost"]
        if o["pool"] and o["free"]:
            ends = fin.setdefault(o["pool"], []) + [done[i] + WAKE]
            fin[o["pool"]] = ends
            if len(ends) == o["free"]:
                slot[o["pool"][0]][held.pop(o["pool"])] = max(fin.pop(o["pool"]))
        order.append(i)
        for x in succ[i]:
            need[x] -= 1
            if not need[x]:
                ready.append(x)
    assert len(order) == n
    order.sort(key=lambda i: start[i])
    return order, buf, start, done


def emit(g, T, ops, order, buf):
    eng = {"V": g.vector, "S": g.scalar, "P": g.tensor, "Q": g.sync, "G": g}
    cnt = {"V": "cV", "S": "cS", "P": "cP", "G": "cG"}
    dep = deps_of(ops, order)
    total, at, after, bank = {}, {}, {}, {}
    clock = {e: {} for e in eng}
    for i in order:
        o = ops[i]
        d = set(dep[i])
        b = buf.get(i)
        if b:
            for k in o["bk"]:
                use = bank.setdefault((b, k), {})
                d.update(v for x, v in use.items() if x != o["eng"])
                use[o["eng"]] = i
        if o["eng"] == "W":
            at[i] = (o["sem"], o["inc"])
            after[i] = {o["sem"]: o["inc"]}
            continue
        e, c = eng[o["eng"]], clock[o["eng"]]
        for k in sorted(d, reverse=True, key=lambda k: (at[k][1], k)):
            if o["eng"] == "P" and ops[k]["eng"] == "P":
                continue
            s, v = at[k]
            if c.get(s, 0) >= v:
                continue
            e.wait_ge(T.sem[s], v)
            for s2, v2 in after[k].items():
                c[s2] = max(c.get(s2, 0), v2)
        r = o["fn"](e, T[b] if b else None)
        s = o["sem"] or cnt[o["eng"]]
        if s != "sent":
            r.then_inc(T.sem[s], o["inc"] or 1)
        total[s] = total.get(s, 0) + (o["inc"] or 1)
        at[i] = (s, total[s])
        after[i] = dict(c)
        after[i][s] = total[s]
    for s in ("cV", "cS", "cP", "cG", "outs", "sent"):
        g.wait_ge(T.sem[s], total[s])


def rank_program(g, core, T, topo):
    rank = T.rank_of(core)
    if rank is None:
        return
    cores = T.cores

    def send(d, out, inp, sem):
        dst = cores[(rank + d) % len(cores)]
        rid, pid = topo.addr(dst)[:2]
        return g.remote_dma(out, inp, T.sem[sem], T.sem["sent"], pid, rid, topo.mask(core, dst))

    ne = len(topo.engines(core, cores[(rank + 1) % len(cores)]))
    ops = graph({"T": T, "send": send, "X": ne})
    order, buf, start, done = plan(ops)
    emit(g, T, ops, order, buf)
